import numpy as np
import ml_dtypes


def mxq(x, axis, fmt="e4m3"):
    dtype, down = {"e4m3": (ml_dtypes.float8_e4m3fn, 7), "e5m2": (ml_dtypes.float8_e5m2, 14)}[fmt]
    v = np.moveaxis(np.asarray(x, np.float32).astype(ml_dtypes.bfloat16).astype(np.float64), axis, -1)
    blocks = v.reshape(v.shape[:-1] + (-1, 32))
    amax = np.abs(blocks).max(-1, keepdims=True)
    byte = np.maximum(np.where(amax > 0, np.frexp(amax)[1] - 1 + 127, 0) - down, 1)
    scale = np.exp2(byte - 127.0)
    codes = (blocks / scale).astype(np.float32).astype(dtype).astype(np.float64)
    return np.moveaxis((codes * scale).reshape(v.shape), -1, axis)


WIDE = False


def mx_kscale(k):
    if not WIDE:
        return np.ones(k)
    levels = np.array([10, -10, 5, -5, 0])
    if k % 512:
        return np.exp2(np.random.permutation(np.resize(levels, k // 32))).repeat(32)
    a = np.empty((k // 512, 16))
    for p in range(k // 512):
        a[p, :8] = np.random.permutation(np.resize(levels, 8))
        for g in range(8):
            far = levels[np.abs(levels - a[p, g]) >= 10]
            a[p, g + 8] = far[np.random.randint(len(far))]
    return np.exp2(a.ravel()).repeat(32)


def f64(x):
    return np.asarray(x).astype(np.float64)


def striped(idx):
    return np.tile(idx.reshape(-1, 16).T, (8, 1)).astype(np.uint16)


def unstriped(offs):
    return offs[:16].T.reshape(-1).astype(np.int64)


def pack_weight(w):
    k, n = w.shape
    w = f64(np.asarray(w, np.float32).astype(ml_dtypes.bfloat16)).reshape(k // 32, 32, n)
    amax = np.abs(w).max(1)
    byte = np.clip(np.where(amax > 0, np.frexp(amax)[1] - 1 + 127 - 7, 1), 1, 254)
    scaled = (w * np.exp2(127.0 - byte)[:, None, :]).reshape(k, n).astype(np.float32)
    words = np.ascontiguousarray(scaled.reshape(k // 512, 128, 4, n).transpose(0, 1, 3, 2)).astype(ml_dtypes.float8_e4m3fn).view(np.uint8)
    return words, np.ascontiguousarray(byte.astype(np.uint8).reshape(k // 512, 16, n))


def unpack_weight(words, scales):
    g, p, n, _ = words.shape
    vals = np.ascontiguousarray(words).view(ml_dtypes.float8_e4m3fn).astype(np.float64) * np.repeat(np.exp2(scales.astype(np.float64) - 127.0), 8, axis=1)[..., None]
    return vals.transpose(0, 1, 3, 2).reshape(g * 512, n)


K, T, D, S, V, N = 1536, 1024, 4, 512, 256, 512


def setup_inputs():
    n = np.random.standard_normal
    s = mx_kscale(K)[:, None]
    words, scales = pack_weight(n((K, N)) / np.sqrt(K) / s)
    return {
        "xT": (n((K, T)) * s).astype(np.float32),
        "w_words": words,
        "w_scales": scales,
        "b": (0.3 * n((N, 1))).astype(np.float32),
        "gate": np.tile(np.random.uniform(0.2, 1.0, (D, 1, V)) / np.sqrt(D), (1, N, 1)).astype(np.float32),
        "offs": striped(np.random.permutation(T)[:S]),
        "pos1": striped(np.random.permutation(S)[:V]),
        "pos2": striped(np.random.permutation(S)[:V]),
        "pos3": striped(np.random.permutation(S)[:V]),
        "pos4": striped(np.random.permutation(S)[:V]),
    }


def reference(xT, w_words, w_scales, b, gate, offs, pos1, pos2, pos3, pos4):
    w = unpack_weight(w_words, w_scales)
    idx = unstriped(offs)
    xq = mxq(f64(xT)[:, idx], 0, "e4m3")
    y = w.T @ xq
    y = y + f64(b)
    return sum(f64(gate[d]) * y[:, unstriped(p)] for d, p in enumerate((pos1, pos2, pos3, pos4)))

@@ -1,0 +1,185 @@
+from contextlib import ExitStack
+
+import concourse.mybir as mybir
+from concourse.masks import make_identity
+
+K, T, D, S, V, N = 1536, 1024, 4, 512, 256, 512
+FLOPS = 2 * K * S * N
+
+F32 = mybir.dt.float32
+BF16 = mybir.dt.bfloat16
+I32 = mybir.dt.int32
+U32 = mybir.dt.uint32
+U16 = mybir.dt.uint16
+U8 = mybir.dt.uint8
+FP8X4 = mybir.dt.float8_e4m3fn_x4
+IDENT = mybir.ActivationFunctionType.Identity
+MULT = mybir.AluOpType.mult
+ADD = mybir.AluOpType.add
+
+P = 128
+PASSES = K // 512
+BLOCKS = N // P
+HALF_T = T // 2
+HALF_S = S // 2
+V_COLS = [[736], [672], [704], [480], [0, 288], [0, 416]]
+
+
+def tile_picked_sub_lin_bias_sub_e_kernel(
+    tc, xT, w_words, w_scales, b, gate, offs, pos1, pos2, pos3, pos4, out
+):
+    nc = tc.nc
+    with ExitStack() as ctx:
+        keep = ctx.enter_context(tc.tile_pool(name="keep", bufs=1))
+        psum = ctx.enter_context(tc.psum_pool(name="psum", bufs=2))
+
+        offs_t = keep.tile([P, S // 16], U16, name="offs_t")
+        pos_t = [keep.tile([P, V // 16], U16, name=f"pos_t{d}") for d in range(D)]
+        w_t = [keep.tile([P, PASSES, P], U32, name=f"w_t{c}", align_bytes=64) for c in range(BLOCKS)]
+        ws_t = keep.tile([P, PASSES, N], U8, name="ws_t", align_bytes=64)
+        bias_t = keep.tile([P, BLOCKS], F32, name="bias_t")
+        ident = keep.tile([P, P], F32, name="ident")
+        warm = keep.tile([P, 2], F32, name="warm")
+
+        nc.vector.memset(ws_t[:].rearrange("p a m -> p (a m)").bitcast(I32), 0)
+        nc.vector.memset(warm[:, 0:1], 0.0)
+        nc.scalar.activation(out=warm[:, 1:2], in_=warm[:, 0:1], func=IDENT)
+        make_identity(nc, ident[:])
+
+        x_view = xT.rearrange("(a p u e) t -> a u p e t", a=PASSES, p=P, u=2, e=2)
+        raw = {}
+        for ch in range(2 * PASSES):
+            parts = len(V_COLS[ch])
+            width = T // parts
+            for h in range(parts):
+                raw[ch, h] = keep.tile([P, 2, width], F32, name=f"raw{ch}{h}")
+                nc.sync.dma_start(out=raw[ch, h][:], in_=x_view[ch // 2, ch % 2, :, :, h * width : (h + 1) * width])
+            if ch == 0:
+                nc.sync.dma_start(offs_t[:], offs)
+        for q in range(4):
+            nc.scalar.dma_start(
+                out=ws_t[32 * q : 32 * q + 4, :, :].bitcast(I32),
+                in_=w_scales[:, 4 * q : 4 * q + 4, :].rearrange("a r m -> r a m").bitcast(I32),
+            )
+        w_view = w_words.rearrange("a p (c m) r -> c p a (m r)", c=BLOCKS)
+        gate_t = []
+        for c in range(BLOCKS):
+            nc.sync.dma_start(out=w_t[c][:].bitcast(I32), in_=w_view[c].bitcast(I32))
+            if c == 0:
+                with nc.allow_non_contiguous_dma(reason="one bias value a partition and block"):
+                    nc.sync.dma_start(out=bias_t[:], in_=b.rearrange("(c p) o -> p (c o)", p=P))
+                for d, pos in enumerate((pos1, pos2, pos3, pos4)):
+                    nc.sync.dma_start(pos_t[d][:], pos)
+            g = keep.tile([P, D, V], F32, name=f"gate{c}")
+            nc.sync.dma_start(out=g[:], in_=gate[:, c * P : (c + 1) * P, :].rearrange("d p v -> p d v"))
+            gate_t.append(g)
+
+        picked = [keep.tile([P, 2, S, 2], BF16, name=f"picked{a}") for a in range(PASSES)]
+        grouped = [keep.tile([P, S, 2, 2], BF16, name=f"grouped{a}", align_bytes=64) for a in range(PASSES)]
+        codes = [keep.tile([P, S], U32, name=f"codes{a}", align_bytes=64) for a in range(PASSES)]
+        scales = [keep.tile([P, S], U8, name=f"scales{a}", align_bytes=64) for a in range(PASSES)]
+        pairs = [keep.tile([P, T, 2], BF16, name=f"pairs{ch}") for ch in range(2 * PASSES)]
+        halves = [(0, HALF_S), (HALF_S, S)]
+
+        def cast(ch):
+            width = T // len(V_COLS[ch])
+            for h, v_cols in enumerate(V_COLS[ch]):
+                src = raw[ch, h][:].rearrange("p e t -> p t e")
+                dst = pairs[ch][:, h * width : (h + 1) * width, :]
+                if v_cols > 0:
+                    nc.vector.tensor_copy(out=dst[:, :v_cols, :], in_=src[:, :v_cols, :])
+                if v_cols < width:
+                    nc.scalar.copy(out=dst[:, v_cols:, :], in_=src[:, v_cols:, :])
+
+        def pick(ch, lo, hi):
+            window = pairs[ch][:].rearrange("p t e -> p (t e)").bitcast(U32)
+            nc.vector.tensor_copy(
+                out=picked[ch // 2][:, ch % 2, lo:hi, :].rearrange("p n e -> p (n e)").bitcast(U32),
+                in_=window.indirect(offs_t[:, lo // 16 : hi // 16]),
+            )
+
+        def interleave(a, lo, hi, copy):
+            copy(out=grouped[a][:, lo:hi], in_=picked[a][:, :, lo:hi, :].rearrange("p u n e -> p n u e"))
+
+        def quantize(a, lo, hi):
+            nc.vector.quantize_mx(
+                out=codes[a][:, lo:hi].bitcast(FP8X4),
+                scales=scales[a][:, lo:hi],
+                in_=grouped[a][:, lo:hi].rearrange("p n u e -> p (n u e)"),
+            )
+
+        for ch in range(2 * PASSES - 1):
+            cast(ch)
+            if ch in (2, 4):
+                interleave(ch // 2 - 1, 0, S, nc.scalar.copy)
+            pick(ch, 0, S)
+            if ch in (2, 4):
+                quantize(ch // 2 - 1, 0, S)
+        cast(2 * PASSES - 1)
+        for lo, hi in halves:
+            pick(2 * PASSES - 1, lo, hi)
+        for lo, hi in halves:
+            interleave(PASSES - 1, lo, hi, nc.vector.tensor_copy)
+        for lo, hi in halves:
+            quantize(PASSES - 1, lo, hi)
+
+        y = []
+        for c in range(BLOCKS):
+            yc = keep.tile([P, S], F32, name=f"y{c}")
+            y.append(yc)
+            cuts = [(0, HALF_S), (HALF_S, S)] if c == 0 else [(0, S)]
+            for lo, hi in cuts:
+                acc = psum.tile([P, S], F32, name="acc")
+                for a in range(PASSES):
+                    nc.tensor.matmul_mx(
+                        out=acc[:, : hi - lo],
+                        lhsT=w_t[c][:, a, :].bitcast(FP8X4),
+                        lhsT_scale=ws_t[:, a, c * P : (c + 1) * P],
+                        rhs=codes[a][:, lo:hi].bitcast(FP8X4),
+                        rhs_scale=scales[a][:, lo:hi],
+                        start=(a == 0),
+                        stop=(a == PASSES - 1),
+                    )
+                nc.scalar.activation(
+                    out=yc[:, lo:hi], in_=acc[:, : hi - lo], func=IDENT, bias=bias_t[:, c : c + 1]
+                )
+
+        prod = [keep.tile([P, D, V], F32, name=f"prod{c}") for c in range(BLOCKS)]
+
+        def weigh(c, d):
+            nc.vector.tensor_tensor(prod[c][:, d, :], y[c][:].indirect(pos_t[d][:]), gate_t[c][:, d, :], MULT)
+
+        def sum_on_tensor(c, terms):
+            turned = [psum.tile([P, P], F32, name=f"turned{half}", bufs=1) for half in range(V // P)]
+            for d in range(terms):
+                for half in range(V // P):
+                    nc.tensor.matmul(
+                        turned[half][:], lhsT=prod[c][:, d, half * P : (half + 1) * P], rhs=ident[:], is_transpose=True,
+                        start=(d == 0), stop=(d == terms - 1),
+                    )
+            turned_sb = keep.tile([P, V], F32, name=f"turned_sb{c}")
+            for half in range(V // P):
+                nc.scalar.copy(out=turned_sb[:, half * P : (half + 1) * P], in_=turned[half][:])
+            back = psum.tile([P, V], F32, name="back", bufs=3)
+            for half in range(V // P):
+                cols = slice(half * P, (half + 1) * P)
+                nc.tensor.transpose(back[:, cols], turned_sb[:, cols], ident[:])
+            return back
+
+        def store(c, res):
+            nc.sync.dma_start(out=out[c * P : (c + 1) * P, :], in_=res[:])
+
+        res = [keep.tile([P, V], F32, name=f"res{c}") for c in range(BLOCKS)]
+        back = {}
+        for c, terms in ((0, D), (1, D - 1), (2, D - 1), (3, D)):
+            for d in range(terms):
+                weigh(c, d)
+            back[c] = sum_on_tensor(c, terms)
+            if terms == D:
+                nc.scalar.copy(out=res[c][:], in_=back[c][:, :V])
+                store(c, res[c])
+        for c in (1, 2):
+            weigh(c, D - 1)
+        for c in (1, 2):
+            nc.vector.tensor_tensor(res[c][:], back[c][:, :V], prod[c][:, D - 1, :], ADD)
+            store(c, res[c])

@@ -22,7 +22,7 @@ PASSES = K // 512
 BLOCKS = N // P
 HALF_T = T // 2
 HALF_S = S // 2
-V_COLS = [[736], [672], [704], [480], [0, 288], [0, 416]]
+V_COLS = [[704], [0, 320], [0, 0], [0, 0], [0, 0], [0, 352]]
 
 
 def tile_picked_sub_lin_bias_sub_e_kernel(
@@ -35,18 +35,29 @@ def tile_picked_sub_lin_bias_sub_e_kernel(
 
         offs_t = keep.tile([P, S // 16], U16, name="offs_t")
         pos_t = [keep.tile([P, V // 16], U16, name=f"pos_t{d}") for d in range(D)]
-        w_t = [keep.tile([P, PASSES, P], U32, name=f"w_t{c}", align_bytes=64) for c in range(BLOCKS)]
-        ws_t = keep.tile([P, PASSES, N], U8, name="ws_t", align_bytes=64)
+        w_first = keep.tile([P, PASSES, P], U32, name="w_first", align_bytes=64)
+        w_rest = keep.tile([P, PASSES, N - P], U32, name="w_rest", align_bytes=64)
+        w_t = [w_first[:]] + [w_rest[:, :, c * P : (c + 1) * P] for c in range(BLOCKS - 1)]
+        ws_t = keep.tile([P, N], U8, name="ws_t", align_bytes=64)
         bias_t = keep.tile([P, BLOCKS], F32, name="bias_t")
         ident = keep.tile([P, P], F32, name="ident")
         warm = keep.tile([P, 2], F32, name="warm")
 
-        nc.vector.memset(ws_t[:].rearrange("p a m -> p (a m)").bitcast(I32), 0)
+        nc.vector.memset(ws_t[:].bitcast(I32), 0)
         nc.vector.memset(warm[:, 0:1], 0.0)
         nc.scalar.activation(out=warm[:, 1:2], in_=warm[:, 0:1], func=IDENT)
+        bias_rows = keep.tile([P, P], F32, name="bias_rows")
+        nc.gpsimd.memset(bias_rows[:], 0.0)
         make_identity(nc, ident[:])
 
         x_view = xT.rearrange("(a p u e) t -> a u p e t", a=PASSES, p=P, u=2, e=2)
+        small = [(offs_t[:], offs)]
+        for q in range(4):
+            small.append((
+                ws_t[32 * q : 32 * q + 4 * PASSES, :].bitcast(I32),
+                w_scales[:, 4 * q : 4 * q + 4, :].bitcast(I32),
+            ))
+        small.append((bias_rows[:BLOCKS, :], b.rearrange("(c p) o -> c (p o)", p=P)))
         raw = {}
         for ch in range(2 * PASSES):
             parts = len(V_COLS[ch])
@@ -54,25 +65,25 @@ def tile_picked_sub_lin_bias_sub_e_kernel(
             for h in range(parts):
                 raw[ch, h] = keep.tile([P, 2, width], F32, name=f"raw{ch}{h}")
                 nc.sync.dma_start(out=raw[ch, h][:], in_=x_view[ch // 2, ch % 2, :, :, h * width : (h + 1) * width])
-            if ch == 0:
-                nc.sync.dma_start(offs_t[:], offs)
-        for q in range(4):
-            nc.scalar.dma_start(
-                out=ws_t[32 * q : 32 * q + 4, :, :].bitcast(I32),
-                in_=w_scales[:, 4 * q : 4 * q + 4, :].rearrange("a r m -> r a m").bitcast(I32),
-            )
-        w_view = w_words.rearrange("a p (c m) r -> c p a (m r)", c=BLOCKS)
-        gate_t = []
-        for c in range(BLOCKS):
-            nc.sync.dma_start(out=w_t[c][:].bitcast(I32), in_=w_view[c].bitcast(I32))
-            if c == 0:
-                with nc.allow_non_contiguous_dma(reason="one bias value a partition and block"):
-                    nc.sync.dma_start(out=bias_t[:], in_=b.rearrange("(c p) o -> p (c o)", p=P))
-                for d, pos in enumerate((pos1, pos2, pos3, pos4)):
-                    nc.sync.dma_start(pos_t[d][:], pos)
-            g = keep.tile([P, D, V], F32, name=f"gate{c}")
-            nc.sync.dma_start(out=g[:], in_=gate[:, c * P : (c + 1) * P, :].rearrange("d p v -> p d v"))
-            gate_t.append(g)
+                if small:
+                    nc.sync.dma_start(*small.pop(0))
+        w_view = w_words.rearrange("a p m r -> p a (m r)").bitcast(I32)
+        gate_t = [keep.tile([P, D, V], F32, name=f"gate{c}") for c in range(BLOCKS)]
+
+        def load_gate(c):
+            nc.sync.dma_start(out=gate_t[c][:], in_=gate[:, c * P : (c + 1) * P, :].rearrange("d p v -> p d v"))
+
+        nc.sync.dma_start(out=w_first[:].bitcast(I32), in_=w_view[:, :, :P])
+        nc.sync.dma_start(out=w_rest[:].bitcast(I32), in_=w_view[:, :, P:])
+        nc.sync.dma_start(pos_t[0][:], pos1)
+        load_gate(0)
+        for d, pos in ((1, pos2), (2, pos3), (3, pos4)):
+            nc.sync.dma_start(pos_t[d][:], pos)
+        for c in (1, 2, 3):
+            load_gate(c)
+        bias_ps = psum.tile([P, V], F32, name="back", bufs=3)
+        nc.tensor.transpose(bias_ps[:, :P], bias_rows[:], ident[:])
+        nc.scalar.copy(out=bias_t[:], in_=bias_ps[:, :BLOCKS])
 
         picked = [keep.tile([P, 2, S, 2], BF16, name=f"picked{a}") for a in range(PASSES)]
         grouped = [keep.tile([P, S, 2, 2], BF16, name=f"grouped{a}", align_bytes=64) for a in range(PASSES)]
@@ -108,20 +119,16 @@ def tile_picked_sub_lin_bias_sub_e_kernel(
                 in_=grouped[a][:, lo:hi].rearrange("p n u e -> p (n u e)"),
             )
 
-        for ch in range(2 * PASSES - 1):
-            cast(ch)
-            if ch in (2, 4):
-                interleave(ch // 2 - 1, 0, S, nc.scalar.copy)
-            pick(ch, 0, S)
-            if ch in (2, 4):
-                quantize(ch // 2 - 1, 0, S)
-        cast(2 * PASSES - 1)
-        for lo, hi in halves:
-            pick(2 * PASSES - 1, lo, hi)
-        for lo, hi in halves:
-            interleave(PASSES - 1, lo, hi, nc.vector.tensor_copy)
-        for lo, hi in halves:
-            quantize(PASSES - 1, lo, hi)
+        for a in range(PASSES):
+            cast(2 * a)
+            pick(2 * a, 0, S)
+            cast(2 * a + 1)
+            for lo, hi in halves:
+                pick(2 * a + 1, lo, hi)
+            for lo, hi in halves:
+                interleave(a, lo, hi, nc.vector.tensor_copy)
+            for lo, hi in halves:
+                quantize(a, lo, hi)
 
         y = []
         for c in range(BLOCKS):
@@ -129,12 +136,12 @@ def tile_picked_sub_lin_bias_sub_e_kernel(
             y.append(yc)
             cuts = [(0, HALF_S), (HALF_S, S)] if c == 0 else [(0, S)]
             for lo, hi in cuts:
-                acc = psum.tile([P, S], F32, name="acc")
+                acc = psum.tile([P, S], F32, name="acc", bufs=2)
                 for a in range(PASSES):
                     nc.tensor.matmul_mx(
                         out=acc[:, : hi - lo],
                         lhsT=w_t[c][:, a, :].bitcast(FP8X4),
-                        lhsT_scale=ws_t[:, a, c * P : (c + 1) * P],
+                        lhsT_scale=ws_t[4 * a :, c * P : (c + 1) * P],
                         rhs=codes[a][:, lo:hi].bitcast(FP8X4),
                         rhs_scale=scales[a][:, lo:hi],
                         start=(a == 0),
@@ -170,16 +177,19 @@ def tile_picked_sub_lin_bias_sub_e_kernel(
             nc.sync.dma_start(out=out[c * P : (c + 1) * P, :], in_=res[:])
 
         res = [keep.tile([P, V], F32, name=f"res{c}") for c in range(BLOCKS)]
-        back = {}
-        for c, terms in ((0, D), (1, D - 1), (2, D - 1), (3, D)):
-            for d in range(terms):
+        for c in range(BLOCKS - 1):
+            for d in range(D):
                 weigh(c, d)
-            back[c] = sum_on_tensor(c, terms)
-            if terms == D:
-                nc.scalar.copy(out=res[c][:], in_=back[c][:, :V])
-                store(c, res[c])
-        for c in (1, 2):
-            weigh(c, D - 1)
-        for c in (1, 2):
-            nc.vector.tensor_tensor(res[c][:], back[c][:, :V], prod[c][:, D - 1, :], ADD)
+            back = sum_on_tensor(c, D)
+            nc.scalar.copy(out=res[c][:], in_=back[:])
             store(c, res[c])
+        c = BLOCKS - 1
+        partial = keep.tile([P, 2, V], F32, name="partial")
+        weigh(c, 0)
+        weigh(c, 1)
+        weigh(c, 2)
+        nc.vector.tensor_tensor(partial[:, 0, :], prod[c][:, 0, :], prod[c][:, 1, :], ADD)
+        weigh(c, 3)
+        nc.vector.tensor_tensor(partial[:, 1, :], partial[:, 0, :], prod[c][:, 2, :], ADD)
+        nc.vector.tensor_tensor(res[c][:], partial[:, 1, :], prod[c][:, 3, :], ADD)
+        store(c, res[c])

@@ -20,9 +20,15 @@ ADD = mybir.AluOpType.add
 P = 128
 PASSES = K // 512
 BLOCKS = N // P
-HALF_T = T // 2
 HALF_S = S // 2
-V_COLS = [[704], [0, 320], [0, 0], [0, 0], [0, 0], [0, 352]]
+LOADS = [
+    [(1024, 672)],
+    [(1024, 640)],
+    [(1024, 256)],
+    [(1024, 384)],
+    [(512, 0), (512, 0)],
+    [(512, 0), (512, 192)],
+]
 
 
 def tile_picked_sub_lin_bias_sub_e_kernel(
@@ -31,19 +37,17 @@ def tile_picked_sub_lin_bias_sub_e_kernel(
     nc = tc.nc
     with ExitStack() as ctx:
         keep = ctx.enter_context(tc.tile_pool(name="keep", bufs=1))
-        psum = ctx.enter_context(tc.psum_pool(name="psum", bufs=2))
+        psum = ctx.enter_context(tc.psum_pool(name="psum", bufs=1))
 
         offs_t = keep.tile([P, S // 16], U16, name="offs_t")
         pos_t = [keep.tile([P, V // 16], U16, name=f"pos_t{d}") for d in range(D)]
-        w_first = keep.tile([P, PASSES, P], U32, name="w_first", align_bytes=64)
-        w_rest = keep.tile([P, PASSES, N - P], U32, name="w_rest", align_bytes=64)
-        w_t = [w_first[:]] + [w_rest[:, :, c * P : (c + 1) * P] for c in range(BLOCKS - 1)]
-        ws_t = keep.tile([P, N], U8, name="ws_t", align_bytes=64)
+        w_t = [keep.tile([P, N], U32, name=f"w_t{a}", align_bytes=64) for a in range(PASSES)]
+        ws_t = keep.tile([P, PASSES, N], U8, name="ws_t", align_bytes=64)
         bias_t = keep.tile([P, BLOCKS], F32, name="bias_t")
         ident = keep.tile([P, P], F32, name="ident")
         warm = keep.tile([P, 2], F32, name="warm")
 
-        nc.vector.memset(ws_t[:].bitcast(I32), 0)
+        nc.vector.memset(ws_t[:].rearrange("p a m -> p (a m)").bitcast(I32), 0)
         nc.vector.memset(warm[:, 0:1], 0.0)
         nc.scalar.activation(out=warm[:, 1:2], in_=warm[:, 0:1], func=IDENT)
         bias_rows = keep.tile([P, P], F32, name="bias_rows")
@@ -51,145 +55,171 @@ def tile_picked_sub_lin_bias_sub_e_kernel(
         make_identity(nc, ident[:])
 
         x_view = xT.rearrange("(a p u e) t -> a u p e t", a=PASSES, p=P, u=2, e=2)
-        small = [(offs_t[:], offs)]
-        for q in range(4):
-            small.append((
-                ws_t[32 * q : 32 * q + 4 * PASSES, :].bitcast(I32),
-                w_scales[:, 4 * q : 4 * q + 4, :].bitcast(I32),
-            ))
-        small.append((bias_rows[:BLOCKS, :], b.rearrange("(c p) o -> c (p o)", p=P)))
         raw = {}
-        for ch in range(2 * PASSES):
-            parts = len(V_COLS[ch])
-            width = T // parts
-            for h in range(parts):
+        for ch, parts in enumerate(LOADS):
+            col = 0
+            for h, (width, v_cols) in enumerate(parts):
                 raw[ch, h] = keep.tile([P, 2, width], F32, name=f"raw{ch}{h}")
-                nc.sync.dma_start(out=raw[ch, h][:], in_=x_view[ch // 2, ch % 2, :, :, h * width : (h + 1) * width])
-                if small:
-                    nc.sync.dma_start(*small.pop(0))
-        w_view = w_words.rearrange("a p m r -> p a (m r)").bitcast(I32)
-        gate_t = [keep.tile([P, D, V], F32, name=f"gate{c}") for c in range(BLOCKS)]
+                nc.sync.dma_start(out=raw[ch, h][:], in_=x_view[ch // 2, ch % 2, :, :, col : col + width])
+                col += width
+            if ch == 0:
+                nc.sync.dma_start(offs_t[:], offs)
+            if ch == 0:
+                nc.sync.dma_start(bias_rows[:BLOCKS, :], b.rearrange("(c p) o -> c (p o)", p=P))
+        for q in range(4):
+            nc.sync.dma_start(
+                out=ws_t[32 * q : 32 * q + 4].bitcast(I32),
+                in_=w_scales[:, 4 * q : 4 * q + 4, :].rearrange("a r m -> r a m").bitcast(I32),
+            )
+        w_view = [w_words[a].rearrange("p m r -> p (m r)").bitcast(I32) for a in range(PASSES)]
+        gate_t = [keep.tile([P, 2, V], F32, name=f"gate{g}") for g in range(D // 2)]
 
-        def load_gate(c):
-            nc.sync.dma_start(out=gate_t[c][:], in_=gate[:, c * P : (c + 1) * P, :].rearrange("d p v -> p d v"))
+        def load_gate(g):
+            nc.sync.dma_start(out=gate_t[g][:], in_=gate[2 * g : 2 * g + 2, :P, :].rearrange("d p v -> p d v"))
 
-        nc.sync.dma_start(out=w_first[:].bitcast(I32), in_=w_view[:, :, :P])
-        nc.sync.dma_start(out=w_rest[:].bitcast(I32), in_=w_view[:, :, P:])
+        for a in range(PASSES):
+            nc.sync.dma_start(out=w_t[a][:].bitcast(I32), in_=w_view[a])
         nc.sync.dma_start(pos_t[0][:], pos1)
+        nc.sync.dma_start(pos_t[1][:], pos2)
         load_gate(0)
-        for d, pos in ((1, pos2), (2, pos3), (3, pos4)):
-            nc.sync.dma_start(pos_t[d][:], pos)
-        for c in (1, 2, 3):
-            load_gate(c)
-        bias_ps = psum.tile([P, V], F32, name="back", bufs=3)
-        nc.tensor.transpose(bias_ps[:, :P], bias_rows[:], ident[:])
+        nc.sync.dma_start(pos_t[2][:], pos3)
+        nc.sync.dma_start(pos_t[3][:], pos4)
+        load_gate(1)
+
+        bias_ps = psum.tile([P, P], F32, name="bank7")
+        nc.tensor.transpose(bias_ps[:], bias_rows[:], ident[:])
         nc.scalar.copy(out=bias_t[:], in_=bias_ps[:, :BLOCKS])
 
-        picked = [keep.tile([P, 2, S, 2], BF16, name=f"picked{a}") for a in range(PASSES)]
-        grouped = [keep.tile([P, S, 2, 2], BF16, name=f"grouped{a}", align_bytes=64) for a in range(PASSES)]
+        slices = [[(lo, lo + width) for lo in range(0, S, width)] for width in (HALF_S, HALF_S, P)]
+        picked = [keep.tile([P, 2, S], U32, name=f"picked{a}") for a in range(PASSES)]
+        grouped = [
+            [keep.tile([P, hi - lo, 2], U32, name=f"grouped{a}{lo}", align_bytes=64) for lo, hi in slices[a]]
+            for a in range(PASSES)
+        ]
         codes = [keep.tile([P, S], U32, name=f"codes{a}", align_bytes=64) for a in range(PASSES)]
         scales = [keep.tile([P, S], U8, name=f"scales{a}", align_bytes=64) for a in range(PASSES)]
         pairs = [keep.tile([P, T, 2], BF16, name=f"pairs{ch}") for ch in range(2 * PASSES)]
-        halves = [(0, HALF_S), (HALF_S, S)]
 
         def cast(ch):
-            width = T // len(V_COLS[ch])
-            for h, v_cols in enumerate(V_COLS[ch]):
+            col = 0
+            for h, (width, v_cols) in enumerate(LOADS[ch]):
                 src = raw[ch, h][:].rearrange("p e t -> p t e")
-                dst = pairs[ch][:, h * width : (h + 1) * width, :]
+                dst = pairs[ch][:, col : col + width, :]
                 if v_cols > 0:
                     nc.vector.tensor_copy(out=dst[:, :v_cols, :], in_=src[:, :v_cols, :])
                 if v_cols < width:
                     nc.scalar.copy(out=dst[:, v_cols:, :], in_=src[:, v_cols:, :])
+                col += width
 
         def pick(ch, lo, hi):
             window = pairs[ch][:].rearrange("p t e -> p (t e)").bitcast(U32)
             nc.vector.tensor_copy(
-                out=picked[ch // 2][:, ch % 2, lo:hi, :].rearrange("p n e -> p (n e)").bitcast(U32),
-                in_=window.indirect(offs_t[:, lo // 16 : hi // 16]),
+                out=picked[ch // 2][:, ch % 2, lo:hi], in_=window.indirect(offs_t[:, lo // 16 : hi // 16])
             )
 
-        def interleave(a, lo, hi, copy):
-            copy(out=grouped[a][:, lo:hi], in_=picked[a][:, :, lo:hi, :].rearrange("p u n e -> p n u e"))
+        def interleave(a, h):
+            lo, hi = slices[a][h]
+            src = picked[a][:, :, lo:hi]
+            if a == PASSES - 1:
+                nc.scalar.copy(out=grouped[a][h][:], in_=src.rearrange("p u n -> p n u"))
+            else:
+                nc.vector.tensor_copy(out=grouped[a][h][:].bitcast(I32), in_=src.bitcast(I32).rearrange("p u n -> p n u"))
 
-        def quantize(a, lo, hi):
+        def quantize(a, h):
+            lo, hi = slices[a][h]
             nc.vector.quantize_mx(
                 out=codes[a][:, lo:hi].bitcast(FP8X4),
                 scales=scales[a][:, lo:hi],
-                in_=grouped[a][:, lo:hi].rearrange("p n u e -> p (n u e)"),
+                in_=grouped[a][h][:].rearrange("p n u -> p (n u)").bitcast(BF16),
             )
 
         for a in range(PASSES):
             cast(2 * a)
             pick(2 * a, 0, S)
             cast(2 * a + 1)
-            for lo, hi in halves:
+            for lo, hi in slices[a]:
                 pick(2 * a + 1, lo, hi)
-            for lo, hi in halves:
-                interleave(a, lo, hi, nc.vector.tensor_copy)
-            for lo, hi in halves:
-                quantize(a, lo, hi)
+            for h in range(len(slices[a])):
+                interleave(a, h)
+            for h in range(len(slices[a])):
+                quantize(a, h)
 
-        y = []
-        for c in range(BLOCKS):
-            yc = keep.tile([P, S], F32, name=f"y{c}")
-            y.append(yc)
-            cuts = [(0, HALF_S), (HALF_S, S)] if c == 0 else [(0, S)]
-            for lo, hi in cuts:
-                acc = psum.tile([P, S], F32, name="acc", bufs=2)
-                for a in range(PASSES):
-                    nc.tensor.matmul_mx(
-                        out=acc[:, : hi - lo],
-                        lhsT=w_t[c][:, a, :].bitcast(FP8X4),
-                        lhsT_scale=ws_t[4 * a :, c * P : (c + 1) * P],
-                        rhs=codes[a][:, lo:hi].bitcast(FP8X4),
-                        rhs_scale=scales[a][:, lo:hi],
-                        start=(a == 0),
-                        stop=(a == PASSES - 1),
-                    )
-                nc.scalar.activation(
-                    out=yc[:, lo:hi], in_=acc[:, : hi - lo], func=IDENT, bias=bias_t[:, c : c + 1]
-                )
+        groups = [(0, 0, HALF_S), (0, HALF_S, S - P), (0, S - P, S)] + [(c, 0, S) for c in range(1, BLOCKS)]
+        acc = {}
+        y = [keep.tile([P, S], F32, name=f"y{c}") for c in range(2)]
 
-        prod = [keep.tile([P, D, V], F32, name=f"prod{c}") for c in range(BLOCKS)]
+        def product(g, a):
+            c, lo, hi = groups[g]
+            if a == 0:
+                acc[g] = psum.tile([P, hi - lo], F32, name=f"bank{g % 4}")
+            nc.tensor.matmul_mx(
+                out=acc[g][:],
+                lhsT=w_t[a][:, c * P : (c + 1) * P].bitcast(FP8X4),
+                lhsT_scale=ws_t[:, a, c * P : (c + 1) * P],
+                rhs=codes[a][:, lo:hi].bitcast(FP8X4),
+                rhs_scale=scales[a][:, lo:hi],
+                start=(a == 0),
+                stop=(a == PASSES - 1),
+            )
+            if a == PASSES - 1 and g == 2:
+                nc.vector.tensor_scalar(out=y[c][:, lo:hi], in0=acc[g][:], scalar1=bias_t[:, c : c + 1], scalar2=None, op0=ADD)
+            elif a == PASSES - 1 and c < 2:
+                nc.scalar.activation(out=y[c][:, lo:hi], in_=acc[g][:], func=IDENT, bias=bias_t[:, c : c + 1])
+
+        for a in range(PASSES):
+            for g in range(4):
+                product(g, a)
+        for g in range(4, len(groups)):
+            for a in range(PASSES):
+                product(g, a)
+
+        prod = [[None] * D for c in range(BLOCKS)]
 
         def weigh(c, d):
-            nc.vector.tensor_tensor(prod[c][:, d, :], y[c][:].indirect(pos_t[d][:]), gate_t[c][:, d, :], MULT)
+            slot = (BLOCKS - 1, 0) if (c, d) == (BLOCKS - 2, D - 1) else (c, d)
+            prod[c][d] = keep.tile([P, V], F32, name=f"prod{slot[0]}{slot[1]}")
+            nc.vector.tensor_tensor(prod[c][d][:], y[c][:].indirect(pos_t[d][:]), gate_t[d // 2][:, d % 2, :], MULT)
 
         def sum_on_tensor(c, terms):
-            turned = [psum.tile([P, P], F32, name=f"turned{half}", bufs=1) for half in range(V // P)]
+            banks = ("bank5", "bank6") if c % 2 == 0 else ("bank2", "bank4")
+            turned = [psum.tile([P, P], F32, name=banks[half]) for half in range(V // P)]
             for d in range(terms):
                 for half in range(V // P):
                     nc.tensor.matmul(
-                        turned[half][:], lhsT=prod[c][:, d, half * P : (half + 1) * P], rhs=ident[:], is_transpose=True,
+                        turned[half][:], lhsT=prod[c][d][:, half * P : (half + 1) * P], rhs=ident[:], is_transpose=True,
                         start=(d == 0), stop=(d == terms - 1),
                     )
             turned_sb = keep.tile([P, V], F32, name=f"turned_sb{c}")
             for half in range(V // P):
                 nc.scalar.copy(out=turned_sb[:, half * P : (half + 1) * P], in_=turned[half][:])
-            back = psum.tile([P, V], F32, name="back", bufs=3)
+            back = psum.tile([P, V], F32, name="bank7" if c % 2 == 0 else "bank3")
             for half in range(V // P):
                 cols = slice(half * P, (half + 1) * P)
                 nc.tensor.transpose(back[:, cols], turned_sb[:, cols], ident[:])
             return back
 
-        def store(c, res):
-            nc.sync.dma_start(out=out[c * P : (c + 1) * P, :], in_=res[:])
+        def empty(c, slot):
+            y.append(keep.tile([P, S], F32, name=slot))
+            nc.scalar.activation(out=y[c][:], in_=acc[c + 2][:], func=IDENT, bias=bias_t[:, c : c + 1])
+
+        def store(c):
+            nc.sync.dma_start(out=out[c * P : (c + 1) * P, :], in_=res[c][:])
 
         res = [keep.tile([P, V], F32, name=f"res{c}") for c in range(BLOCKS)]
-        for c in range(BLOCKS - 1):
+        for c in range(BLOCKS - 2):
             for d in range(D):
                 weigh(c, d)
             back = sum_on_tensor(c, D)
+            empty(c + 2, f"prod{c}0")
             nc.scalar.copy(out=res[c][:], in_=back[:])
-            store(c, res[c])
-        c = BLOCKS - 1
-        partial = keep.tile([P, 2, V], F32, name="partial")
-        weigh(c, 0)
-        weigh(c, 1)
-        weigh(c, 2)
-        nc.vector.tensor_tensor(partial[:, 0, :], prod[c][:, 0, :], prod[c][:, 1, :], ADD)
-        weigh(c, 3)
-        nc.vector.tensor_tensor(partial[:, 1, :], partial[:, 0, :], prod[c][:, 2, :], ADD)
-        nc.vector.tensor_tensor(res[c][:], partial[:, 1, :], prod[c][:, 3, :], ADD)
-        store(c, res[c])
+            store(c)
+        backs = {}
+        for c in range(BLOCKS - 2, BLOCKS):
+            for d in range(D - 1):
+                weigh(c, d)
+            backs[c] = sum_on_tensor(c, D - 1)
+        for c in range(BLOCKS - 2, BLOCKS):
+            weigh(c, D - 1)
+        for c in range(BLOCKS - 2, BLOCKS):
+            nc.vector.tensor_tensor(res[c][:], backs[c][:], prod[c][D - 1][:], ADD)
+            store(c)

@@ -64,8 +64,7 @@ def tile_picked_sub_lin_bias_sub_e_kernel(
                 col += width
             if ch == 0:
                 nc.sync.dma_start(offs_t[:], offs)
-            if ch == 0:
-                nc.sync.dma_start(bias_rows[:BLOCKS, :], b.rearrange("(c p) o -> c (p o)", p=P))
+        nc.sync.dma_start(bias_rows[:BLOCKS, :], b.rearrange("(c p) o -> c (p o)", p=P))
         for q in range(4):
             nc.sync.dma_start(
                 out=ws_t[32 * q : 32 * q + 4].bitcast(I32),
@@ -176,7 +175,7 @@ def tile_picked_sub_lin_bias_sub_e_kernel(
         prod = [[None] * D for c in range(BLOCKS)]
 
         def weigh(c, d):
-            slot = (BLOCKS - 1, 0) if (c, d) == (BLOCKS - 2, D - 1) else (c, d)
+            slot = (BLOCKS - 1, c - (BLOCKS - 2)) if c >= BLOCKS - 2 and d == D - 1 else (c, d)
             prod[c][d] = keep.tile([P, V], F32, name=f"prod{slot[0]}{slot[1]}")
             nc.vector.tensor_tensor(prod[c][d][:], y[c][:].indirect(pos_t[d][:]), gate_t[d // 2][:, d % 2, :], MULT)
 
@@ -192,10 +191,13 @@ def tile_picked_sub_lin_bias_sub_e_kernel(
             turned_sb = keep.tile([P, V], F32, name=f"turned_sb{c}")
             for half in range(V // P):
                 nc.scalar.copy(out=turned_sb[:, half * P : (half + 1) * P], in_=turned[half][:])
-            back = psum.tile([P, V], F32, name="bank7" if c % 2 == 0 else "bank3")
+            if c == BLOCKS - 1:
+                back = [psum.tile([P, P], F32, name=name)[:] for name in ("bank3", "bank1")]
+            else:
+                whole = psum.tile([P, V], F32, name="bank7" if c % 2 == 0 else "bank3")
+                back = [whole[:, half * P : (half + 1) * P] for half in range(V // P)] + [whole[:]]
             for half in range(V // P):
-                cols = slice(half * P, (half + 1) * P)
-                nc.tensor.transpose(back[:, cols], turned_sb[:, cols], ident[:])
+                nc.tensor.transpose(back[half], turned_sb[:, half * P : (half + 1) * P], ident[:])
             return back
 
         def empty(c, slot):
@@ -211,7 +213,7 @@ def tile_picked_sub_lin_bias_sub_e_kernel(
                 weigh(c, d)
             back = sum_on_tensor(c, D)
             empty(c + 2, f"prod{c}0")
-            nc.scalar.copy(out=res[c][:], in_=back[:])
+            nc.scalar.copy(out=res[c][:], in_=back[2])
             store(c)
         backs = {}
         for c in range(BLOCKS - 2, BLOCKS):
@@ -220,6 +222,11 @@ def tile_picked_sub_lin_bias_sub_e_kernel(
             backs[c] = sum_on_tensor(c, D - 1)
         for c in range(BLOCKS - 2, BLOCKS):
             weigh(c, D - 1)
-        for c in range(BLOCKS - 2, BLOCKS):
-            nc.vector.tensor_tensor(res[c][:], backs[c][:], prod[c][D - 1][:], ADD)
-            store(c)
+        c = BLOCKS - 2
+        nc.vector.tensor_tensor(res[c][:], backs[c][2], prod[c][D - 1][:], ADD)
+        store(c)
+        c = BLOCKS - 1
+        for half in range(V // P):
+            cols = slice(half * P, (half + 1) * P)
+            nc.vector.tensor_tensor(res[c][:, cols], backs[c][half], prod[c][D - 1][:, cols], ADD)
+            nc.sync.dma_start(out=out[c * P : (c + 1) * P, cols], in_=res[c][:, cols])

@@ -19,15 +19,18 @@ ADD = mybir.AluOpType.add
 
 P = 128
 PASSES = K // 512
+LAST_PASS = PASSES - 1
 BLOCKS = N // P
 HALF_S = S // 2
+QUARTER_S = S // 4
+V_HALVES = [slice(0, P), slice(P, V)]
 LOADS = [
     [(1024, 672)],
     [(1024, 640)],
-    [(1024, 256)],
-    [(1024, 384)],
     [(512, 0), (512, 0)],
-    [(512, 0), (512, 192)],
+    [(512, 0), (512, 256)],
+    [(512, 0), (512, 0)],
+    [(512, 0), (512, 320)],
 ]
 
 
@@ -42,191 +45,205 @@ def tile_picked_sub_lin_bias_sub_e_kernel(
         offs_t = keep.tile([P, S // 16], U16, name="offs_t")
         pos_t = [keep.tile([P, V // 16], U16, name=f"pos_t{d}") for d in range(D)]
         w_t = [keep.tile([P, N], U32, name=f"w_t{a}", align_bytes=64) for a in range(PASSES)]
-        ws_t = keep.tile([P, PASSES, N], U8, name="ws_t", align_bytes=64)
+        ws_t = keep.tile([P, N], U8, name="ws_t", align_bytes=64)
         bias_t = keep.tile([P, BLOCKS], F32, name="bias_t")
         ident = keep.tile([P, P], F32, name="ident")
         warm = keep.tile([P, 2], F32, name="warm")
 
-        nc.vector.memset(ws_t[:].rearrange("p a m -> p (a m)").bitcast(I32), 0)
+        nc.vector.memset(ws_t[:].bitcast(I32), 0)
         nc.vector.memset(warm[:, 0:1], 0.0)
         nc.scalar.activation(out=warm[:, 1:2], in_=warm[:, 0:1], func=IDENT)
         bias_rows = keep.tile([P, P], F32, name="bias_rows")
-        nc.gpsimd.memset(bias_rows[:], 0.0)
+        nc.vector.memset(bias_rows[:], 0.0)
         make_identity(nc, ident[:])
+        for q in range(4):
+            nc.gpsimd.dma_start(
+                out=ws_t[32 * q : 32 * q + 4 * PASSES].bitcast(I32),
+                in_=w_scales[:, 4 * q : 4 * q + 4, :].bitcast(I32),
+            )
 
         x_view = xT.rearrange("(a p u e) t -> a u p e t", a=PASSES, p=P, u=2, e=2)
         raw = {}
-        for ch, parts in enumerate(LOADS):
+        for pair, pieces in enumerate(LOADS):
             col = 0
-            for h, (width, v_cols) in enumerate(parts):
-                raw[ch, h] = keep.tile([P, 2, width], F32, name=f"raw{ch}{h}")
-                nc.sync.dma_start(out=raw[ch, h][:], in_=x_view[ch // 2, ch % 2, :, :, col : col + width])
+            for piece, (width, _) in enumerate(pieces):
+                raw[pair, piece] = keep.tile([P, 2, width], F32, name=f"raw{pair}{piece}")
+                nc.sync.dma_start(out=raw[pair, piece][:], in_=x_view[pair // 2, pair % 2, :, :, col : col + width])
                 col += width
-            if ch == 0:
+            if pair == 0:
                 nc.sync.dma_start(offs_t[:], offs)
         nc.sync.dma_start(bias_rows[:BLOCKS, :], b.rearrange("(c p) o -> c (p o)", p=P))
-        for q in range(4):
-            nc.sync.dma_start(
-                out=ws_t[32 * q : 32 * q + 4].bitcast(I32),
-                in_=w_scales[:, 4 * q : 4 * q + 4, :].rearrange("a r m -> r a m").bitcast(I32),
-            )
         w_view = [w_words[a].rearrange("p m r -> p (m r)").bitcast(I32) for a in range(PASSES)]
         gate_t = [keep.tile([P, 2, V], F32, name=f"gate{g}") for g in range(D // 2)]
-
-        def load_gate(g):
-            nc.sync.dma_start(out=gate_t[g][:], in_=gate[2 * g : 2 * g + 2, :P, :].rearrange("d p v -> p d v"))
-
         for a in range(PASSES):
             nc.sync.dma_start(out=w_t[a][:].bitcast(I32), in_=w_view[a])
-        nc.sync.dma_start(pos_t[0][:], pos1)
-        nc.sync.dma_start(pos_t[1][:], pos2)
-        load_gate(0)
-        nc.sync.dma_start(pos_t[2][:], pos3)
-        nc.sync.dma_start(pos_t[3][:], pos4)
-        load_gate(1)
+        for g, lists in enumerate(((pos1, pos2), (pos3, pos4))):
+            for e, pos in enumerate(lists):
+                nc.sync.dma_start(pos_t[2 * g + e][:], pos)
+            nc.sync.dma_start(out=gate_t[g][:], in_=gate[2 * g : 2 * g + 2, :P, :].rearrange("d p v -> p d v"))
 
         bias_ps = psum.tile([P, P], F32, name="bank7")
         nc.tensor.transpose(bias_ps[:], bias_rows[:], ident[:])
         nc.scalar.copy(out=bias_t[:], in_=bias_ps[:, :BLOCKS])
 
-        slices = [[(lo, lo + width) for lo in range(0, S, width)] for width in (HALF_S, HALF_S, P)]
+        slices = [[(lo, lo + width) for lo in range(0, S, width)] for width in (HALF_S, HALF_S, QUARTER_S)]
         picked = [keep.tile([P, 2, S], U32, name=f"picked{a}") for a in range(PASSES)]
-        grouped = [
-            [keep.tile([P, hi - lo, 2], U32, name=f"grouped{a}{lo}", align_bytes=64) for lo, hi in slices[a]]
+        last_slice = (LAST_PASS, len(slices[LAST_PASS]) - 1)
+        grouped = {
+            (a, h): keep.tile([P, hi - lo, 2], U32, name=f"grouped{a}{lo}", align_bytes=64)
             for a in range(PASSES)
-        ]
+            for h, (lo, hi) in enumerate(slices[a])
+            if (a, h) != last_slice
+        }
         codes = [keep.tile([P, S], U32, name=f"codes{a}", align_bytes=64) for a in range(PASSES)]
         scales = [keep.tile([P, S], U8, name=f"scales{a}", align_bytes=64) for a in range(PASSES)]
-        pairs = [keep.tile([P, T, 2], BF16, name=f"pairs{ch}") for ch in range(2 * PASSES)]
+        rounded = [keep.tile([P, T, 2], BF16, name=f"rounded{pair}") for pair in range(2 * PASSES)]
 
-        def cast(ch):
+        def round_pair(pair):
             col = 0
-            for h, (width, v_cols) in enumerate(LOADS[ch]):
-                src = raw[ch, h][:].rearrange("p e t -> p t e")
-                dst = pairs[ch][:, col : col + width, :]
+            for piece, (width, v_cols) in enumerate(LOADS[pair]):
+                src = raw[pair, piece][:].rearrange("p e t -> p t e")
+                dst = rounded[pair][:, col : col + width, :]
                 if v_cols > 0:
                     nc.vector.tensor_copy(out=dst[:, :v_cols, :], in_=src[:, :v_cols, :])
-                if v_cols < width:
-                    nc.scalar.copy(out=dst[:, v_cols:, :], in_=src[:, v_cols:, :])
+                nc.scalar.copy(out=dst[:, v_cols:, :], in_=src[:, v_cols:, :])
                 col += width
 
-        def pick(ch, lo, hi):
-            window = pairs[ch][:].rearrange("p t e -> p (t e)").bitcast(U32)
+        def pick(pair, lo, hi):
+            window = rounded[pair][:].rearrange("p t e -> p (t e)").bitcast(U32)
             nc.vector.tensor_copy(
-                out=picked[ch // 2][:, ch % 2, lo:hi], in_=window.indirect(offs_t[:, lo // 16 : hi // 16])
+                out=picked[pair // 2][:, pair % 2, lo:hi], in_=window.indirect(offs_t[:, lo // 16 : hi // 16])
             )
 
-        def interleave(a, h):
+        def interleave(a, h, on_scalar):
             lo, hi = slices[a][h]
             src = picked[a][:, :, lo:hi]
-            if a == PASSES - 1:
-                nc.scalar.copy(out=grouped[a][h][:], in_=src.rearrange("p u n -> p n u"))
+            if on_scalar:
+                nc.scalar.copy(out=grouped[a, h][:], in_=src.rearrange("p u n -> p n u"))
             else:
-                nc.vector.tensor_copy(out=grouped[a][h][:].bitcast(I32), in_=src.bitcast(I32).rearrange("p u n -> p n u"))
+                nc.vector.tensor_copy(
+                    out=grouped[a, h][:].bitcast(I32), in_=src.bitcast(I32).rearrange("p u n -> p n u")
+                )
 
         def quantize(a, h):
             lo, hi = slices[a][h]
             nc.vector.quantize_mx(
                 out=codes[a][:, lo:hi].bitcast(FP8X4),
                 scales=scales[a][:, lo:hi],
-                in_=grouped[a][h][:].rearrange("p n u -> p (n u)").bitcast(BF16),
+                in_=grouped[a, h][:].rearrange("p n u -> p (n u)").bitcast(BF16),
             )
 
         for a in range(PASSES):
-            cast(2 * a)
+            round_pair(2 * a)
             pick(2 * a, 0, S)
-            cast(2 * a + 1)
+            round_pair(2 * a + 1)
             for lo, hi in slices[a]:
                 pick(2 * a + 1, lo, hi)
-            for h in range(len(slices[a])):
-                interleave(a, h)
-            for h in range(len(slices[a])):
-                quantize(a, h)
+            if a < LAST_PASS:
+                for h in range(len(slices[a])):
+                    interleave(a, h, on_scalar=False)
+                for h in range(len(slices[a])):
+                    quantize(a, h)
+        last_h = last_slice[1]
+        for h in range(last_h):
+            interleave(LAST_PASS, h, on_scalar=True)
+        quantize(LAST_PASS, 0)
+        grouped[last_slice] = keep.tile([P, QUARTER_S, 2], U32, name=f"grouped{LAST_PASS}0", align_bytes=64)
+        interleave(LAST_PASS, last_h, on_scalar=False)
+        for h in range(1, last_h + 1):
+            quantize(LAST_PASS, h)
 
-        groups = [(0, 0, HALF_S), (0, HALF_S, S - P), (0, S - P, S)] + [(c, 0, S) for c in range(1, BLOCKS)]
+        groups = [(0, 0, HALF_S), (0, HALF_S, S - QUARTER_S), (0, S - QUARTER_S, S)]
+        groups = groups + [(c, 0, S) for c in range(1, BLOCKS)]
+        early_groups = 4
+        third_quarter = 1
         acc = {}
         y = [keep.tile([P, S], F32, name=f"y{c}") for c in range(2)]
 
         def product(g, a):
             c, lo, hi = groups[g]
             if a == 0:
-                acc[g] = psum.tile([P, hi - lo], F32, name=f"bank{g % 4}")
+                acc[g] = psum.tile([P, hi - lo], F32, name=f"bank{g % early_groups}")
             nc.tensor.matmul_mx(
                 out=acc[g][:],
                 lhsT=w_t[a][:, c * P : (c + 1) * P].bitcast(FP8X4),
-                lhsT_scale=ws_t[:, a, c * P : (c + 1) * P],
+                lhsT_scale=ws_t[4 * a :, c * P : (c + 1) * P],
                 rhs=codes[a][:, lo:hi].bitcast(FP8X4),
                 rhs_scale=scales[a][:, lo:hi],
                 start=(a == 0),
-                stop=(a == PASSES - 1),
+                stop=(a == LAST_PASS),
             )
-            if a == PASSES - 1 and g == 2:
-                nc.vector.tensor_scalar(out=y[c][:, lo:hi], in0=acc[g][:], scalar1=bias_t[:, c : c + 1], scalar2=None, op0=ADD)
-            elif a == PASSES - 1 and c < 2:
-                nc.scalar.activation(out=y[c][:, lo:hi], in_=acc[g][:], func=IDENT, bias=bias_t[:, c : c + 1])
+
+        def empty(g):
+            c, lo, hi = groups[g]
+            bias = bias_t[:, c : c + 1]
+            if g == third_quarter:
+                nc.vector.tensor_scalar(out=y[c][:, lo:hi], in0=acc[g][:], scalar1=bias, scalar2=None, op0=ADD)
+            else:
+                nc.scalar.activation(out=y[c][:, lo:hi], in_=acc[g][:], func=IDENT, bias=bias)
 
         for a in range(PASSES):
-            for g in range(4):
+            for g in range(early_groups):
                 product(g, a)
-        for g in range(4, len(groups)):
+                if a == LAST_PASS:
+                    empty(g)
+        for g in range(early_groups, len(groups)):
             for a in range(PASSES):
                 product(g, a)
 
-        prod = [[None] * D for c in range(BLOCKS)]
+        prod = {}
 
-        def weigh(c, d):
-            slot = (BLOCKS - 1, c - (BLOCKS - 2)) if c >= BLOCKS - 2 and d == D - 1 else (c, d)
-            prod[c][d] = keep.tile([P, V], F32, name=f"prod{slot[0]}{slot[1]}")
-            nc.vector.tensor_tensor(prod[c][d][:], y[c][:].indirect(pos_t[d][:]), gate_t[d // 2][:, d % 2, :], MULT)
+        def weigh(c, d, slot):
+            prod[c, d] = keep.tile([P, V], F32, name=slot)
+            nc.vector.tensor_tensor(prod[c, d][:], y[c][:].indirect(pos_t[d][:]), gate_t[d // 2][:, d % 2, :], MULT)
 
-        def sum_on_tensor(c, terms):
+        def turn_and_add(c, terms):
             banks = ("bank5", "bank6") if c % 2 == 0 else ("bank2", "bank4")
-            turned = [psum.tile([P, P], F32, name=banks[half]) for half in range(V // P)]
+            turned = [psum.tile([P, P], F32, name=bank) for bank in banks]
             for d in range(terms):
-                for half in range(V // P):
+                for half, cols in enumerate(V_HALVES):
                     nc.tensor.matmul(
-                        turned[half][:], lhsT=prod[c][d][:, half * P : (half + 1) * P], rhs=ident[:], is_transpose=True,
+                        turned[half][:], lhsT=prod[c, d][:, cols], rhs=ident[:], is_transpose=True,
                         start=(d == 0), stop=(d == terms - 1),
                     )
             turned_sb = keep.tile([P, V], F32, name=f"turned_sb{c}")
-            for half in range(V // P):
-                nc.scalar.copy(out=turned_sb[:, half * P : (half + 1) * P], in_=turned[half][:])
-            if c == BLOCKS - 1:
-                back = [psum.tile([P, P], F32, name=name)[:] for name in ("bank3", "bank1")]
-            else:
-                whole = psum.tile([P, V], F32, name="bank7" if c % 2 == 0 else "bank3")
-                back = [whole[:, half * P : (half + 1) * P] for half in range(V // P)] + [whole[:]]
-            for half in range(V // P):
-                nc.tensor.transpose(back[half], turned_sb[:, half * P : (half + 1) * P], ident[:])
+            for half, cols in enumerate(V_HALVES):
+                nc.scalar.copy(out=turned_sb[:, cols], in_=turned[half][:])
+            return turned_sb
+
+        def turn_back(turned_sb, bank):
+            back = psum.tile([P, V], F32, name=bank)
+            for cols in V_HALVES:
+                nc.tensor.transpose(back[:, cols], turned_sb[:, cols], ident[:])
             return back
 
-        def empty(c, slot):
-            y.append(keep.tile([P, S], F32, name=slot))
-            nc.scalar.activation(out=y[c][:], in_=acc[c + 2][:], func=IDENT, bias=bias_t[:, c : c + 1])
-
-        def store(c):
-            nc.sync.dma_start(out=out[c * P : (c + 1) * P, :], in_=res[c][:])
+        def store(c, cols):
+            nc.sync.dma_start(out=out[c * P : (c + 1) * P, cols], in_=res[c][:, cols])
 
         res = [keep.tile([P, V], F32, name=f"res{c}") for c in range(BLOCKS)]
-        for c in range(BLOCKS - 2):
+        all_cols = slice(0, V)
+        for c, bank in enumerate(("bank7", "bank3")):
             for d in range(D):
-                weigh(c, d)
-            back = sum_on_tensor(c, D)
-            empty(c + 2, f"prod{c}0")
-            nc.scalar.copy(out=res[c][:], in_=back[2])
-            store(c)
-        backs = {}
-        for c in range(BLOCKS - 2, BLOCKS):
-            for d in range(D - 1):
-                weigh(c, d)
-            backs[c] = sum_on_tensor(c, D - 1)
-        for c in range(BLOCKS - 2, BLOCKS):
-            weigh(c, D - 1)
-        c = BLOCKS - 2
-        nc.vector.tensor_tensor(res[c][:], backs[c][2], prod[c][D - 1][:], ADD)
-        store(c)
-        c = BLOCKS - 1
-        for half in range(V // P):
-            cols = slice(half * P, (half + 1) * P)
-            nc.vector.tensor_tensor(res[c][:, cols], backs[c][half], prod[c][D - 1][:, cols], ADD)
-            nc.sync.dma_start(out=out[c * P : (c + 1) * P, cols], in_=res[c][:, cols])
+                weigh(c, d, f"prod{c}{d}")
+            back = turn_back(turn_and_add(c, D), bank)
+            y.append(keep.tile([P, S], F32, name=f"prod{c}0"))
+            empty(early_groups + c)
+            nc.scalar.copy(out=res[c][:], in_=back[:])
+            store(c, all_cols)
+        second_last, last = BLOCKS - 2, BLOCKS - 1
+        for d in range(D - 1):
+            weigh(second_last, d, f"prod{second_last}{d}")
+        back_second_last = turn_back(turn_and_add(second_last, D - 1), "bank7")
+        for d in range(D - 1):
+            weigh(last, d, f"prod{last}{d}")
+        turned_last = turn_and_add(last, D - 1)
+        back_last = [psum.tile([P, P], F32, name=bank) for bank in ("bank3", "bank1")]
+        for half, cols in enumerate(V_HALVES):
+            nc.tensor.transpose(back_last[half][:], turned_last[:, cols], ident[:])
+        weigh(second_last, D - 1, f"prod{last}0")
+        weigh(last, D - 1, f"prod{last}1")
+        nc.vector.tensor_tensor(res[second_last][:], back_second_last[:], prod[second_last, D - 1][:], ADD)
+        store(second_last, all_cols)
+        for half, cols in enumerate(V_HALVES):
+            nc.vector.tensor_tensor(res[last][:, cols], back_last[half][:], prod[last, D - 1][:, cols], ADD)
+            store(last, cols)

@@ -14,6 +14,7 @@ U16 = mybir.dt.uint16
 U8 = mybir.dt.uint8
 FP8X4 = mybir.dt.float8_e4m3fn_x4
 IDENT = mybir.ActivationFunctionType.Identity
+COPY = mybir.ActivationFunctionType.Copy
 MULT = mybir.AluOpType.mult
 ADD = mybir.AluOpType.add
 
@@ -24,14 +25,9 @@ BLOCKS = N // P
 HALF_S = S // 2
 QUARTER_S = S // 4
 V_HALVES = [slice(0, P), slice(P, V)]
-LOADS = [
-    [(1024, 672)],
-    [(1024, 640)],
-    [(512, 0), (512, 0)],
-    [(512, 0), (512, 256)],
-    [(512, 0), (512, 0)],
-    [(512, 0), (512, 320)],
-]
+PLANES = 4
+RUN = 4
+VECTOR_SHARE = [[0, 0, S, 0], [0, 0, S, 0], [0, 0, S - QUARTER_S, QUARTER_S]]
 
 
 def tile_picked_sub_lin_bias_sub_e_kernel(
@@ -62,24 +58,25 @@ def tile_picked_sub_lin_bias_sub_e_kernel(
                 in_=w_scales[:, 4 * q : 4 * q + 4, :].bitcast(I32),
             )
 
-        x_view = xT.rearrange("(a p u e) t -> a u p e t", a=PASSES, p=P, u=2, e=2)
+        x_view = xT.rearrange("(a p t) n -> a p t n", a=PASSES, p=P, t=PLANES)
         raw = {}
-        for pair, pieces in enumerate(LOADS):
-            col = 0
-            for piece, (width, _) in enumerate(pieces):
-                raw[pair, piece] = keep.tile([P, 2, width], F32, name=f"raw{pair}{piece}")
-                nc.sync.dma_start(out=raw[pair, piece][:], in_=x_view[pair // 2, pair % 2, :, :, col : col + width])
-                col += width
-            if pair == 0:
-                nc.sync.dma_start(offs_t[:], offs)
-        nc.sync.dma_start(bias_rows[:BLOCKS, :], b.rearrange("(c p) o -> c (p o)", p=P))
+        for a in range(PASSES):
+            step = 1 if a == LAST_PASS else 2
+            for first in range(0, PLANES, step):
+                rows = keep.tile([P, step, T], F32, name=f"raw{a}{first}")
+                nc.sync.dma_start(out=rows[:], in_=x_view[a, :, first : first + step, :])
+                for t in range(first, first + step):
+                    raw[a, t] = rows[:, t - first, :]
+                if (a, first) == (0, 0):
+                    nc.sync.dma_start(offs_t[:], offs)
+                    nc.sync.dma_start(bias_rows[:BLOCKS, :], b.rearrange("(c p) o -> c (p o)", p=P))
         w_view = [w_words[a].rearrange("p m r -> p (m r)").bitcast(I32) for a in range(PASSES)]
         gate_t = [keep.tile([P, 2, V], F32, name=f"gate{g}") for g in range(D // 2)]
+        for d, pos in enumerate((pos1, pos2, pos3, pos4)):
+            nc.sync.dma_start(pos_t[d][:], pos)
         for a in range(PASSES):
             nc.sync.dma_start(out=w_t[a][:].bitcast(I32), in_=w_view[a])
-        for g, lists in enumerate(((pos1, pos2), (pos3, pos4))):
-            for e, pos in enumerate(lists):
-                nc.sync.dma_start(pos_t[2 * g + e][:], pos)
+        for g in range(D // 2):
             nc.sync.dma_start(out=gate_t[g][:], in_=gate[2 * g : 2 * g + 2, :P, :].rearrange("d p v -> p d v"))
 
         bias_ps = psum.tile([P, P], F32, name="bank7")
@@ -87,91 +84,84 @@ def tile_picked_sub_lin_bias_sub_e_kernel(
         nc.scalar.copy(out=bias_t[:], in_=bias_ps[:, :BLOCKS])
 
         slices = [[(lo, lo + width) for lo in range(0, S, width)] for width in (HALF_S, HALF_S, QUARTER_S)]
-        picked = [keep.tile([P, 2, S], U32, name=f"picked{a}") for a in range(PASSES)]
-        last_slice = (LAST_PASS, len(slices[LAST_PASS]) - 1)
+        picked = [keep.tile([P, PLANES, S], F32, name=f"picked{a}") for a in range(PASSES)]
         grouped = {
-            (a, h): keep.tile([P, hi - lo, 2], U32, name=f"grouped{a}{lo}", align_bytes=64)
+            (a, h): keep.tile([P, hi - lo, PLANES], BF16, name=f"grouped{a}{lo}", align_bytes=64)
             for a in range(PASSES)
             for h, (lo, hi) in enumerate(slices[a])
-            if (a, h) != last_slice
         }
         codes = [keep.tile([P, S], U32, name=f"codes{a}", align_bytes=64) for a in range(PASSES)]
         scales = [keep.tile([P, S], U8, name=f"scales{a}", align_bytes=64) for a in range(PASSES)]
-        rounded = [keep.tile([P, T, 2], BF16, name=f"rounded{pair}") for pair in range(2 * PASSES)]
 
-        def round_pair(pair):
-            col = 0
-            for piece, (width, v_cols) in enumerate(LOADS[pair]):
-                src = raw[pair, piece][:].rearrange("p e t -> p t e")
-                dst = rounded[pair][:, col : col + width, :]
-                if v_cols > 0:
-                    nc.vector.tensor_copy(out=dst[:, :v_cols, :], in_=src[:, :v_cols, :])
-                nc.scalar.copy(out=dst[:, v_cols:, :], in_=src[:, v_cols:, :])
-                col += width
-
-        def pick(pair, lo, hi):
-            window = rounded[pair][:].rearrange("p t e -> p (t e)").bitcast(U32)
-            nc.vector.tensor_copy(
-                out=picked[pair // 2][:, pair % 2, lo:hi], in_=window.indirect(offs_t[:, lo // 16 : hi // 16])
-            )
+        def pick(a, t, lo, hi, on_scalar):
+            window = raw[a, t].indirect(offs_t[:, lo // 16 : hi // 16])
+            if on_scalar:
+                nc.scalar.activation(picked[a][:, t, lo:hi], window, COPY)
+            else:
+                nc.vector.tensor_copy(out=picked[a][:, t, lo:hi], in_=window)
 
         def interleave(a, h, on_scalar):
             lo, hi = slices[a][h]
-            src = picked[a][:, :, lo:hi]
+            src = picked[a][:, :, lo:hi].rearrange("p t (c i) -> p c t i", i=RUN)
+            dst = grouped[a, h][:].rearrange("p (c i) t -> p c t i", i=RUN)
             if on_scalar:
-                nc.scalar.copy(out=grouped[a, h][:], in_=src.rearrange("p u n -> p n u"))
+                nc.scalar.copy(out=dst, in_=src)
             else:
-                nc.vector.tensor_copy(
-                    out=grouped[a, h][:].bitcast(I32), in_=src.bitcast(I32).rearrange("p u n -> p n u")
-                )
+                nc.vector.tensor_copy(out=dst, in_=src)
 
         def quantize(a, h):
             lo, hi = slices[a][h]
             nc.vector.quantize_mx(
                 out=codes[a][:, lo:hi].bitcast(FP8X4),
                 scales=scales[a][:, lo:hi],
-                in_=grouped[a, h][:].rearrange("p n u -> p (n u)").bitcast(BF16),
+                in_=grouped[a, h][:].rearrange("p n t -> p (n t)"),
             )
 
         for a in range(PASSES):
-            round_pair(2 * a)
-            pick(2 * a, 0, S)
-            round_pair(2 * a + 1)
-            for lo, hi in slices[a]:
-                pick(2 * a + 1, lo, hi)
+            for t in range(PLANES):
+                share = VECTOR_SHARE[a][t]
+                if share > 0:
+                    pick(a, t, 0, share, on_scalar=False)
+                if (a, t) == (LAST_PASS, PLANES - 1):
+                    for lo, hi in slices[a][1:]:
+                        pick(a, t, lo, hi, on_scalar=True)
+                elif share < S:
+                    pick(a, t, share, S, on_scalar=True)
             if a < LAST_PASS:
                 for h in range(len(slices[a])):
                     interleave(a, h, on_scalar=False)
                 for h in range(len(slices[a])):
                     quantize(a, h)
-        last_h = last_slice[1]
-        for h in range(last_h):
-            interleave(LAST_PASS, h, on_scalar=True)
+        last_quarter = len(slices[LAST_PASS]) - 1
+        interleave(LAST_PASS, last_quarter, on_scalar=True)
+        interleave(LAST_PASS, 0, on_scalar=False)
+        interleave(LAST_PASS, 1, on_scalar=False)
         quantize(LAST_PASS, 0)
-        grouped[last_slice] = keep.tile([P, QUARTER_S, 2], U32, name=f"grouped{LAST_PASS}0", align_bytes=64)
-        interleave(LAST_PASS, last_h, on_scalar=False)
-        for h in range(1, last_h + 1):
+        interleave(LAST_PASS, 2, on_scalar=False)
+        for h in range(1, last_quarter + 1):
             quantize(LAST_PASS, h)
 
         groups = [(0, 0, HALF_S), (0, HALF_S, S - QUARTER_S), (0, S - QUARTER_S, S)]
+        first_block_groups = len(groups)
         groups = groups + [(c, 0, S) for c in range(1, BLOCKS)]
-        early_groups = 4
+        banks = ["bank0", "bank1", "bank2", "bank3", "bank2", "bank1"]
         third_quarter = 1
         acc = {}
-        y = [keep.tile([P, S], F32, name=f"y{c}") for c in range(2)]
+        y = [keep.tile([P, S], F32, name=f"y{c}") for c in range(BLOCKS)]
 
-        def product(g, a):
+        def product(g, a, closes):
             c, lo, hi = groups[g]
-            if a == 0:
-                acc[g] = psum.tile([P, hi - lo], F32, name=f"bank{g % early_groups}")
+            opens = g not in acc
+            if opens:
+                acc[g] = psum.tile([P, hi - lo], F32, name=banks[g])
             nc.tensor.matmul_mx(
                 out=acc[g][:],
                 lhsT=w_t[a][:, c * P : (c + 1) * P].bitcast(FP8X4),
                 lhsT_scale=ws_t[4 * a :, c * P : (c + 1) * P],
                 rhs=codes[a][:, lo:hi].bitcast(FP8X4),
                 rhs_scale=scales[a][:, lo:hi],
-                start=(a == 0),
-                stop=(a == LAST_PASS),
+                start=opens,
+                stop=closes,
             )
 
         def empty(g):
@@ -183,67 +173,74 @@ def tile_picked_sub_lin_bias_sub_e_kernel(
                 nc.scalar.activation(out=y[c][:, lo:hi], in_=acc[g][:], func=IDENT, bias=bias)
 
         for a in range(PASSES):
-            for g in range(early_groups):
-                product(g, a)
+            for g in range(first_block_groups):
+                product(g, a, a == LAST_PASS)
                 if a == LAST_PASS:
                     empty(g)
-        for g in range(early_groups, len(groups)):
-            for a in range(PASSES):
-                product(g, a)
+        later_order = (LAST_PASS, 0, 1)
+        for g in range(first_block_groups, len(groups)):
+            for a in later_order:
+                product(g, a, a == later_order[-1])
 
-        prod = {}
+        prod = [keep.tile([P, D, V], F32, name=f"prod{c}") for c in range(BLOCKS)]
+        plain = [keep.tile([P, D, V], F32, name=f"plain{c}") for c in range(BLOCKS)]
+        res = [keep.tile([P, V], F32, name=f"res{c}") for c in range(BLOCKS - 1)]
 
-        def weigh(c, d, slot):
-            prod[c, d] = keep.tile([P, V], F32, name=slot)
-            nc.vector.tensor_tensor(prod[c, d][:], y[c][:].indirect(pos_t[d][:]), gate_t[d // 2][:, d % 2, :], MULT)
+        def gates(lo, hi):
+            return gate_t[lo // 2][:, lo % 2 : lo % 2 + hi - lo, :]
 
-        def turn_and_add(c, terms):
-            banks = ("bank5", "bank6") if c % 2 == 0 else ("bank2", "bank4")
-            turned = [psum.tile([P, P], F32, name=bank) for bank in banks]
-            for d in range(terms):
-                for half, cols in enumerate(V_HALVES):
-                    nc.tensor.matmul(
-                        turned[half][:], lhsT=prod[c, d][:, cols], rhs=ident[:], is_transpose=True,
-                        start=(d == 0), stop=(d == terms - 1),
-                    )
-            turned_sb = keep.tile([P, V], F32, name=f"turned_sb{c}")
-            for half, cols in enumerate(V_HALVES):
-                nc.scalar.copy(out=turned_sb[:, cols], in_=turned[half][:])
-            return turned_sb
+        def fetch_weighed(c, d):
+            nc.vector.tensor_tensor(prod[c][:, d, :], y[c][:].indirect(pos_t[d][:]), gates(d, d + 1)[:, 0, :], MULT)
 
-        def turn_back(turned_sb, bank):
-            back = psum.tile([P, V], F32, name=bank)
-            for cols in V_HALVES:
-                nc.tensor.transpose(back[:, cols], turned_sb[:, cols], ident[:])
-            return back
+        def fetch(c, d):
+            nc.scalar.activation(plain[c][:, d, :], y[c][:].indirect(pos_t[d][:]), COPY)
 
-        def store(c, cols):
-            nc.sync.dma_start(out=out[c * P : (c + 1) * P, cols], in_=res[c][:, cols])
+        def weigh(c, lo):
+            nc.vector.tensor_tensor(prod[c][:, lo:, :], plain[c][:, lo:, :], gates(lo, D), MULT)
 
-        res = [keep.tile([P, V], F32, name=f"res{c}") for c in range(BLOCKS)]
-        all_cols = slice(0, V)
-        for c, bank in enumerate(("bank7", "bank3")):
-            for d in range(D):
-                weigh(c, d, f"prod{c}{d}")
-            back = turn_back(turn_and_add(c, D), bank)
-            y.append(keep.tile([P, S], F32, name=f"prod{c}0"))
-            empty(early_groups + c)
+        def add_turned(bank_name, parts):
+            bank = psum.tile([P, V], F32, name=bank_name)
+            for n, (half, source) in enumerate(parts):
+                nc.tensor.matmul(
+                    bank[:, V_HALVES[half]], lhsT=source, rhs=ident[:], is_transpose=True,
+                    start=(n == 0), stop=(n == len(parts) - 1),
+                )
+            return bank
+
+        def store(c):
+            nc.sync.dma_start(out=out[c * P : (c + 1) * P, :], in_=res[c][:])
+
+        last = BLOCKS - 1
+        turned = []
+        for c, bank in enumerate(("bank6", "bank7", "bank5")):
+            fetch(c, 2)
+            fetch(c, 3)
+            empty(first_block_groups + c)
+            fetch_weighed(c, 0)
+            fetch_weighed(c, 1)
+            weigh(c, 2)
+            turned.append(
+                add_turned(bank, [(half, prod[c][:, d, cols]) for d in range(D) for half, cols in enumerate(V_HALVES)])
+            )
+        fetch(last, 3)
+        fetch_weighed(last, 0)
+        fetch_weighed(last, 1)
+        weigh(last, 3)
+        pair_sum = keep.tile([P, V], F32, name="pair_sum")
+        triple_sum = keep.tile([P, V], F32, name="triple_sum")
+        nc.vector.tensor_tensor(pair_sum[:], prod[last][:, 0, :], prod[last][:, 1, :], ADD)
+        fetch_weighed(last, 2)
+        for cols in V_HALVES:
+            nc.vector.tensor_tensor(triple_sum[:, cols], pair_sum[:, cols], prod[last][:, 3, cols], ADD)
+        summed = []
+        for c in range(last):
+            summed.append(keep.tile([P, V], F32, name=f"summed{c}"))
+            nc.scalar.copy(out=summed[c][:], in_=turned[c][:])
+        for c, bank in enumerate(("bank4", "bank0", "bank3")):
+            back = add_turned(bank, [(half, summed[c][:, cols]) for half, cols in enumerate(V_HALVES)])
             nc.scalar.copy(out=res[c][:], in_=back[:])
-            store(c, all_cols)
-        second_last, last = BLOCKS - 2, BLOCKS - 1
-        for d in range(D - 1):
-            weigh(second_last, d, f"prod{second_last}{d}")
-        back_second_last = turn_back(turn_and_add(second_last, D - 1), "bank7")
-        for d in range(D - 1):
-            weigh(last, d, f"prod{last}{d}")
-        turned_last = turn_and_add(last, D - 1)
-        back_last = [psum.tile([P, P], F32, name=bank) for bank in ("bank3", "bank1")]
-        for half, cols in enumerate(V_HALVES):
-            nc.tensor.transpose(back_last[half][:], turned_last[:, cols], ident[:])
-        weigh(second_last, D - 1, f"prod{last}0")
-        weigh(last, D - 1, f"prod{last}1")
-        nc.vector.tensor_tensor(res[second_last][:], back_second_last[:], prod[second_last, D - 1][:], ADD)
-        store(second_last, all_cols)
-        for half, cols in enumerate(V_HALVES):
-            nc.vector.tensor_tensor(res[last][:, cols], back_last[half][:], prod[last, D - 1][:, cols], ADD)
-            store(last, cols)
+            store(c)
+        res.append(keep.tile([P, V], F32, name=f"summed{last - 1}"))
+        for cols in V_HALVES:
+            nc.vector.tensor_tensor(res[last][:, cols], triple_sum[:, cols], prod[last][:, 2, cols], ADD)
+        store(last)

from contextlib import ExitStack

import concourse.mybir as mybir
from concourse.masks import make_identity

K, T, D, S, V, N = 1536, 1024, 4, 512, 256, 512
FLOPS = 2 * K * S * N

F32 = mybir.dt.float32
BF16 = mybir.dt.bfloat16
I32 = mybir.dt.int32
U32 = mybir.dt.uint32
U16 = mybir.dt.uint16
U8 = mybir.dt.uint8
FP8X4 = mybir.dt.float8_e4m3fn_x4
IDENT = mybir.ActivationFunctionType.Identity
COPY = mybir.ActivationFunctionType.Copy
MULT = mybir.AluOpType.mult
ADD = mybir.AluOpType.add

P = 128
PASSES = K // 512
LAST_PASS = PASSES - 1
BLOCKS = N // P
HALF_S = S // 2
QUARTER_S = S // 4
V_HALVES = [slice(0, P), slice(P, V)]
PLANES = 4
RUN = 4
VECTOR_SHARE = [[0, 0, S, 0], [0, 0, S, 0], [0, 0, S - QUARTER_S, QUARTER_S]]


def tile_picked_sub_lin_bias_sub_e_kernel(
    tc, xT, w_words, w_scales, b, gate, offs, pos1, pos2, pos3, pos4, out
):
    nc = tc.nc
    with ExitStack() as ctx:
        keep = ctx.enter_context(tc.tile_pool(name="keep", bufs=1))
        psum = ctx.enter_context(tc.psum_pool(name="psum", bufs=1))

        offs_t = keep.tile([P, S // 16], U16, name="offs_t")
        pos_t = [keep.tile([P, V // 16], U16, name=f"pos_t{d}") for d in range(D)]
        w_t = [keep.tile([P, N], U32, name=f"w_t{a}", align_bytes=64) for a in range(PASSES)]
        ws_t = keep.tile([P, N], U8, name="ws_t", align_bytes=64)
        bias_t = keep.tile([P, BLOCKS], F32, name="bias_t")
        ident = keep.tile([P, P], F32, name="ident")
        warm = keep.tile([P, 2], F32, name="warm")

        nc.vector.memset(ws_t[:].bitcast(I32), 0)
        nc.vector.memset(warm[:, 0:1], 0.0)
        nc.scalar.activation(out=warm[:, 1:2], in_=warm[:, 0:1], func=IDENT)
        bias_rows = keep.tile([P, P], F32, name="bias_rows")
        nc.vector.memset(bias_rows[:], 0.0)
        make_identity(nc, ident[:])
        for q in range(4):
            nc.gpsimd.dma_start(
                out=ws_t[32 * q : 32 * q + 4 * PASSES].bitcast(I32),
                in_=w_scales[:, 4 * q : 4 * q + 4, :].bitcast(I32),
            )

        x_view = xT.rearrange("(a p t) n -> a p t n", a=PASSES, p=P, t=PLANES)
        raw = {}
        for a in range(PASSES):
            step = 1 if a == LAST_PASS else 2
            for first in range(0, PLANES, step):
                rows = keep.tile([P, step, T], F32, name=f"raw{a}{first}")
                nc.sync.dma_start(out=rows[:], in_=x_view[a, :, first : first + step, :])
                for t in range(first, first + step):
                    raw[a, t] = rows[:, t - first, :]
                if (a, first) == (0, 0):
                    nc.sync.dma_start(offs_t[:], offs)
                    nc.sync.dma_start(bias_rows[:BLOCKS, :], b.rearrange("(c p) o -> c (p o)", p=P))
        w_view = [w_words[a].rearrange("p m r -> p (m r)").bitcast(I32) for a in range(PASSES)]
        gate_t = [keep.tile([P, 2, V], F32, name=f"gate{g}") for g in range(D // 2)]
        for d, pos in enumerate((pos1, pos2, pos3, pos4)):
            nc.sync.dma_start(pos_t[d][:], pos)
        for a in range(PASSES):
            nc.sync.dma_start(out=w_t[a][:].bitcast(I32), in_=w_view[a])
        for g in range(D // 2):
            nc.sync.dma_start(out=gate_t[g][:], in_=gate[2 * g : 2 * g + 2, :P, :].rearrange("d p v -> p d v"))

        bias_ps = psum.tile([P, P], F32, name="bank7")
        nc.tensor.transpose(bias_ps[:], bias_rows[:], ident[:])
        nc.scalar.copy(out=bias_t[:], in_=bias_ps[:, :BLOCKS])

        slices = [[(lo, lo + width) for lo in range(0, S, width)] for width in (HALF_S, HALF_S, QUARTER_S)]
        picked = [keep.tile([P, PLANES, S], F32, name=f"picked{a}") for a in range(PASSES)]
        grouped = {
            (a, h): keep.tile([P, hi - lo, PLANES], BF16, name=f"grouped{a}{lo}", align_bytes=64)
            for a in range(PASSES)
            for h, (lo, hi) in enumerate(slices[a])
        }
        codes = [keep.tile([P, S], U32, name=f"codes{a}", align_bytes=64) for a in range(PASSES)]
        scales = [keep.tile([P, S], U8, name=f"scales{a}", align_bytes=64) for a in range(PASSES)]

        def pick(a, t, lo, hi, on_scalar):
            window = raw[a, t].indirect(offs_t[:, lo // 16 : hi // 16])
            if on_scalar:
                nc.scalar.activation(picked[a][:, t, lo:hi], window, COPY)
            else:
                nc.vector.tensor_copy(out=picked[a][:, t, lo:hi], in_=window)

        def interleave(a, h, on_scalar):
            lo, hi = slices[a][h]
            src = picked[a][:, :, lo:hi].rearrange("p t (c i) -> p c t i", i=RUN)
            dst = grouped[a, h][:].rearrange("p (c i) t -> p c t i", i=RUN)
            if on_scalar:
                nc.scalar.copy(out=dst, in_=src)
            else:
                nc.vector.tensor_copy(out=dst, in_=src)

        def quantize(a, h):
            lo, hi = slices[a][h]
            nc.vector.quantize_mx(
                out=codes[a][:, lo:hi].bitcast(FP8X4),
                scales=scales[a][:, lo:hi],
                in_=grouped[a, h][:].rearrange("p n t -> p (n t)"),
            )

        for a in range(PASSES):
            for t in range(PLANES):
                share = VECTOR_SHARE[a][t]
                if share > 0:
                    pick(a, t, 0, share, on_scalar=False)
                if (a, t) == (LAST_PASS, PLANES - 1):
                    for lo, hi in slices[a][1:]:
                        pick(a, t, lo, hi, on_scalar=True)
                elif share < S:
                    pick(a, t, share, S, on_scalar=True)
            if a < LAST_PASS:
                for h in range(len(slices[a])):
                    interleave(a, h, on_scalar=False)
                for h in range(len(slices[a])):
                    quantize(a, h)
        last_quarter = len(slices[LAST_PASS]) - 1
        interleave(LAST_PASS, last_quarter, on_scalar=True)
        interleave(LAST_PASS, 0, on_scalar=False)
        interleave(LAST_PASS, 1, on_scalar=False)
        quantize(LAST_PASS, 0)
        interleave(LAST_PASS, 2, on_scalar=False)
        for h in range(1, last_quarter + 1):
            quantize(LAST_PASS, h)

        groups = [(0, 0, HALF_S), (0, HALF_S, S - QUARTER_S), (0, S - QUARTER_S, S)]
        first_block_groups = len(groups)
        groups = groups + [(c, 0, S) for c in range(1, BLOCKS)]
        banks = ["bank0", "bank1", "bank2", "bank3", "bank2", "bank1"]
        third_quarter = 1
        acc = {}
        y = [keep.tile([P, S], F32, name=f"y{c}") for c in range(BLOCKS)]

        def product(g, a, closes):
            c, lo, hi = groups[g]
            opens = g not in acc
            if opens:
                acc[g] = psum.tile([P, hi - lo], F32, name=banks[g])
            nc.tensor.matmul_mx(
                out=acc[g][:],
                lhsT=w_t[a][:, c * P : (c + 1) * P].bitcast(FP8X4),
                lhsT_scale=ws_t[4 * a :, c * P : (c + 1) * P],
                rhs=codes[a][:, lo:hi].bitcast(FP8X4),
                rhs_scale=scales[a][:, lo:hi],
                start=opens,
                stop=closes,
            )

        def empty(g):
            c, lo, hi = groups[g]
            bias = bias_t[:, c : c + 1]
            if g == third_quarter:
                nc.vector.tensor_scalar(out=y[c][:, lo:hi], in0=acc[g][:], scalar1=bias, scalar2=None, op0=ADD)
            else:
                nc.scalar.activation(out=y[c][:, lo:hi], in_=acc[g][:], func=IDENT, bias=bias)

        for a in range(PASSES):
            for g in range(first_block_groups):
                product(g, a, a == LAST_PASS)
                if a == LAST_PASS:
                    empty(g)
        later_order = (LAST_PASS, 0, 1)
        for g in range(first_block_groups, len(groups)):
            for a in later_order:
                product(g, a, a == later_order[-1])

        prod = [keep.tile([P, D, V], F32, name=f"prod{c}") for c in range(BLOCKS)]
        plain = [keep.tile([P, D, V], F32, name=f"plain{c}") for c in range(BLOCKS)]
        res = [keep.tile([P, V], F32, name=f"res{c}") for c in range(BLOCKS - 1)]

        def gates(lo, hi):
            return gate_t[lo // 2][:, lo % 2 : lo % 2 + hi - lo, :]

        def fetch_weighed(c, d):
            nc.vector.tensor_tensor(prod[c][:, d, :], y[c][:].indirect(pos_t[d][:]), gates(d, d + 1)[:, 0, :], MULT)

        def fetch(c, d):
            nc.scalar.activation(plain[c][:, d, :], y[c][:].indirect(pos_t[d][:]), COPY)

        def weigh(c, lo):
            nc.vector.tensor_tensor(prod[c][:, lo:, :], plain[c][:, lo:, :], gates(lo, D), MULT)

        def add_turned(bank_name, parts):
            bank = psum.tile([P, V], F32, name=bank_name)
            for n, (half, source) in enumerate(parts):
                nc.tensor.matmul(
                    bank[:, V_HALVES[half]], lhsT=source, rhs=ident[:], is_transpose=True,
                    start=(n == 0), stop=(n == len(parts) - 1),
                )
            return bank

        def store(c):
            nc.sync.dma_start(out=out[c * P : (c + 1) * P, :], in_=res[c][:])

        last = BLOCKS - 1
        turned = []
        for c, bank in enumerate(("bank6", "bank7", "bank5")):
            fetch(c, 2)
            fetch(c, 3)
            empty(first_block_groups + c)
            fetch_weighed(c, 0)
            fetch_weighed(c, 1)
            weigh(c, 2)
            turned.append(
                add_turned(bank, [(half, prod[c][:, d, cols]) for d in range(D) for half, cols in enumerate(V_HALVES)])
            )
        fetch(last, 3)
        fetch_weighed(last, 0)
        fetch_weighed(last, 1)
        weigh(last, 3)
        pair_sum = keep.tile([P, V], F32, name="pair_sum")
        triple_sum = keep.tile([P, V], F32, name="triple_sum")
        nc.vector.tensor_tensor(pair_sum[:], prod[last][:, 0, :], prod[last][:, 1, :], ADD)
        fetch_weighed(last, 2)
        for cols in V_HALVES:
            nc.vector.tensor_tensor(triple_sum[:, cols], pair_sum[:, cols], prod[last][:, 3, cols], ADD)
        summed = []
        for c in range(last):
            summed.append(keep.tile([P, V], F32, name=f"summed{c}"))
            nc.scalar.copy(out=summed[c][:], in_=turned[c][:])
        for c, bank in enumerate(("bank4", "bank0", "bank3")):
            back = add_turned(bank, [(half, summed[c][:, cols]) for half, cols in enumerate(V_HALVES)])
            nc.scalar.copy(out=res[c][:], in_=back[:])
            store(c)
        res.append(keep.tile([P, V], F32, name=f"summed{last - 1}"))
        for cols in V_HALVES:
            nc.vector.tensor_tensor(res[last][:, cols], triple_sum[:, cols], prod[last][:, 2, cols], ADD)
        store(last)
